import numpy as np
import ml_dtypes


def mxq(x, axis, fmt="e4m3"):
    dtype, down = {"e4m3": (ml_dtypes.float8_e4m3fn, 7), "e5m2": (ml_dtypes.float8_e5m2, 14)}[fmt]
    v = np.moveaxis(np.asarray(x, np.float32).astype(ml_dtypes.bfloat16).astype(np.float64), axis, -1)
    blocks = v.reshape(v.shape[:-1] + (-1, 32))
    amax = np.abs(blocks).max(-1, keepdims=True)
    byte = np.maximum(np.where(amax > 0, np.frexp(amax)[1] - 1 + 127, 0) - down, 1)
    scale = np.exp2(byte - 127.0)
    codes = (blocks / scale).astype(np.float32).astype(dtype).astype(np.float64)
    return np.moveaxis((codes * scale).reshape(v.shape), -1, axis)


WIDE = False


def mx_kscale(k):
    if not WIDE:
        return np.ones(k)
    levels = np.array([30, -30])
    if k % 512:
        return np.exp2(np.random.permutation(np.resize(levels, k // 32))).repeat(32)
    a = np.empty((k // 512, 16))
    for p in range(k // 512):
        a[p, :8] = np.random.permutation(np.resize(levels, 8))
        for g in range(8):
            far = levels[np.abs(levels - a[p, g]) >= 10]
            a[p, g + 8] = far[np.random.randint(len(far))]
    return np.exp2(a.ravel()).repeat(32)


def f64(x):
    return np.asarray(x).astype(np.float64)


def striped(idx):
    return np.tile(np.asarray(idx).reshape(-1, 16).T, (8, 1)).astype(np.uint16)


def unstriped(offs):
    return offs[:16].T.reshape(-1).astype(np.int64)


def bf(x):
    return np.asarray(x, np.float32).astype(ml_dtypes.bfloat16)


def planes(Y):
    r, m = Y.shape
    b = f64(bf(Y)).reshape(r // 32, 32, m)
    amax = np.abs(b).max(1)
    byte = np.clip(np.where(amax > 0, np.frexp(amax)[1] - 1 + 127 - 7, 1), 1, 254)
    codes = (b * np.exp2(127.0 - byte)[:, None, :]).reshape(r, m).astype(np.float32).astype(ml_dtypes.float8_e4m3fn).view(np.uint8)
    words = codes.reshape(r // 512, 128, 4, m).transpose(0, 1, 3, 2)
    return np.ascontiguousarray(words), np.ascontiguousarray(byte.astype(np.uint8).reshape(r // 512, 16, m))


K, J, N, T, V = 512, 512, 256, 1024, 1024


def setup_inputs():
    n = np.random.standard_normal
    idx = np.random.permutation(T)[:J]
    idx2 = np.random.permutation(V)[:J]
    fj = mx_kscale(J)
    return {
        "xf": (n((K, T))).astype(np.float32),
        "ra": (np.random.uniform(0.5, 1.5, (1, J)) * fj).astype(np.float32),
        "lo": (np.random.uniform(-0.3, 0.5, (K, 1))).astype(np.float32),
        "gt": (n((N, V)) * np.exp(0.5 * n((1, V)))).astype(np.float32),
        "rb": (np.random.uniform(0.5, 1.5, (1, J)) / fj).astype(np.float32),
        "sv": (n((N, V))).astype(np.float32),
        "gk": (np.random.uniform(0.5, 2.0, (K, 1))).astype(np.float32),
        "bn": (np.random.uniform(-12.0, 12.0, (1, N))).astype(np.float32),
        "offs": striped(idx),
        "offs2": striped(idx2),
    }


def reference(xf, ra, lo, gt, rb, sv, gk, bn, offs, offs2):
    idx = unstriped(offs)
    idx2 = unstriped(offs2)
    us = np.maximum(f64(xf)[:, idx] - f64(lo), 0.0) * f64(ra)
    uj = us.T
    gs = f64(gt)[:, idx2] * np.maximum(f64(sv)[:, idx2], 0.0) * f64(rb)
    gj = gs.T
    ujq = mxq(uj, 0, "e5m2")
    gjq = mxq(gj, 0, "e5m2")
    w = ujq.T @ gjq
    wb = w + f64(bn)
    mn = np.mean(wb, axis=1, keepdims=True)
    dw = wb - mn
    y = dw / (np.mean(np.abs(dw), axis=1, keepdims=True) + 2.0) * f64(gk)
    words, scales = planes(y)
    return y, words, scales

@@ -1,0 +1,176 @@
+from contextlib import ExitStack
+
+import concourse.mybir as mybir
+from concourse.masks import make_identity
+
+K, J, N, T, V = 512, 512, 256, 1024, 1024
+FLOPS = 2 * K * J * N
+
+F32 = mybir.dt.float32
+BF16 = mybir.dt.bfloat16
+U32 = mybir.dt.uint32
+I32 = mybir.dt.int32
+U16 = mybir.dt.uint16
+U8 = mybir.dt.uint8
+E5M2X4 = mybir.dt.float8_e5m2_x4
+E4M3X4 = mybir.dt.float8_e4m3fn_x4
+ALU = mybir.AluOpType
+ACT = mybir.ActivationFunctionType
+
+P = 128
+PACK = 4
+HALVES = N // P
+
+
+def tile_list_moment_over_saved_spread_pl_kernel(tc, xf, ra, lo, gt, rb, sv, gk, bn, offs, offs2, out_0, out_1, out_2):
+    nc = tc.nc
+    with ExitStack() as ctx:
+        sb = ctx.enter_context(tc.tile_pool(name="sb", bufs=1))
+        ps = ctx.enter_context(tc.psum_pool(name="ps", bufs=1))
+
+        list_x = sb.tile([P, J // 16], U16, name="list_x")
+        list_g = sb.tile([P, J // 16], U16, name="list_g")
+        sv_win = [sb.tile([P, V], F32, name=f"sv_win{h}") for h in range(HALVES)]
+        gt_win = [sb.tile([P, V], F32, name=f"gt_win{h}") for h in range(HALVES)]
+        x_win = [sb.tile([P, T], F32, name=f"x_win{r}") for r in range(PACK)]
+        ra_t = sb.tile([P, PACK], F32, name="ra_t")
+        rb_t = sb.tile([P, PACK], F32, name="rb_t")
+        lo_t = sb.tile([P, PACK], F32, name="lo_t")
+        gk_t = sb.tile([P, PACK], F32, name="gk_t")
+        bn_t = sb.tile([P, HALVES], F32, name="bn_t")
+        xf_rows = xf.rearrange("(p r) t -> p r t", r=PACK)
+
+        nc.sync.dma_start(lo_t[:], lo.rearrange("(p r) o -> p (r o)", r=PACK))
+        nc.scalar.dma_start(rb_t[:], rb[0].rearrange("(p t) -> p t", t=PACK))
+        nc.sync.dma_start(gt_win[0][:], gt[0:P, :])
+        nc.scalar.dma_start(bn_t[:], bn[0].rearrange("(p e) -> p e", e=HALVES))
+        nc.scalar.dma_start(ra_t[:], ra[0].rearrange("(p t) -> p t", t=PACK))
+        nc.sync.dma_start(list_g[:], offs2)
+        nc.sync.dma_start(sv_win[0][:], sv[0:P, :])
+        nc.sync.dma_start(sv_win[1][:], sv[P : 2 * P, :])
+        nc.sync.dma_start(gt_win[1][:], gt[P : 2 * P, :])
+        nc.sync.dma_start(list_x[:], offs)
+        for r in range(PACK):
+            nc.sync.dma_start(x_win[r][:], xf_rows[:, r, :])
+        nc.sync.dma_start(gk_t[:], gk.rearrange("(p r) o -> p (r o)", r=PACK))
+
+        ident = sb.tile([P, P], F32, name="ident")
+        make_identity(nc, ident[:])
+
+        def along_slots(weights):
+            return weights[:].unsqueeze(1).to_broadcast([P, P, PACK])
+
+        neg_lo = sb.tile([P, PACK], F32, name="neg_lo")
+        nc.scalar.activation(neg_lo[:], lo_t[:], ACT.Copy, scale=-1.0)
+
+        def pick_scalar(window, offsets, name):
+            pick = sb.tile([P, J], F32, name=name, tag=name)
+            nc.scalar.activation(pick[:], window[:].indirect(offsets[:]), ACT.Copy)
+            return [pick[:, t::PACK] for t in range(PACK)]
+
+        def pick_vector(window, offsets, name):
+            pick = sb.tile([P, PACK, P], F32, name=name, tag=name)
+            nc.vector.tensor_copy(pick[:].rearrange("p t q -> p q t"), window[:].indirect(offsets[:]))
+            return [pick[:, t, :] for t in range(PACK)]
+
+        def turn(slots, name, tag):
+            bank = ps.tile([P, PACK, P], F32, name=name, tag=tag)
+            for t in range(PACK):
+                nc.tensor.transpose(bank[:, t, :], slots[t], ident[:])
+            return bank[:].rearrange("q t m -> q m t")
+
+        g_codes = sb.tile([P, N], U32, name="g_codes", align_bytes=64)
+        g_scales = sb.tile([P, N], U8, name="g_scales", align_bytes=64)
+        gt_turned = {0: turn(pick_scalar(gt_win[0], list_g, "gt_pick0"), "gt_bank0", "bank2")}
+        sv_turned = {0: turn(pick_vector(sv_win[0], list_g, "sv_pick0"), "sv_bank0", "bank0")}
+
+        x_bank = [ps.tile([P, PACK, P], F32, name=f"x_bank{r}", tag=f"bank{4 + r}") for r in range(PACK)]
+        for r in range(PACK):
+            for t in range(PACK):
+                nc.tensor.matmul(x_bank[r][:, t, :], neg_lo[:, r : r + 1].to_broadcast([P, P]), ident[:],
+                                 start=(t == 0), stop=False, is_transpose=True)
+        bn_bank = ps.tile([P, HALVES, P], F32, name="bn_bank", tag="bank3")
+        for e in range(HALVES):
+            nc.tensor.transpose(bn_bank[:, e, :], bn_t[:, e : e + 1].to_broadcast([P, P]), ident[:])
+        bn_row = sb.tile([P, P, HALVES], F32, name="bn_row")
+        nc.vector.tensor_scalar(bn_row[:], bn_bank[:].rearrange("q e p -> q p e"), -1.0 / N, None, ALU.mult)
+
+        sv_turned[1] = turn(pick_scalar(sv_win[1], list_g, "sv_pick1"), "sv_bank1", "bank1")
+        gt_turned[1] = turn(pick_scalar(gt_win[1], list_g, "gt_pick1"), "gt_bank1", "bank3")
+        for h in range(HALVES):
+            gate = sb.tile([P, P, PACK], F32, name=f"gate{h}")
+            nc.vector.scalar_tensor_tensor(gate[:], sv_turned[h], 0.0, along_slots(rb_t), ALU.max, ALU.mult)
+            g_bf = sb.tile([P, P, PACK], BF16, name=f"g_bf{h}", align_bytes=64)
+            nc.vector.tensor_tensor(g_bf[:], gt_turned[h], gate[:], ALU.mult)
+            cols = slice(h * P, (h + 1) * P)
+            nc.vector.quantize_mx(g_codes[:, cols].bitcast(E5M2X4), g_scales[:, cols], g_bf[:].rearrange("q m t -> q (m t)"))
+
+        y = sb.tile([P, PACK, N], F32, name="y")
+        out_rows = out_0.rearrange("(p r) n -> p r n", r=PACK)
+        w_bank, u_bf, part, neg_mean = {}, {}, {}, {}
+
+        def weigh(r):
+            slots = pick_scalar(x_win[r], list_x, f"x_pick{r}")
+            for t in range(PACK):
+                nc.tensor.matmul(x_bank[r][:, t, :], slots[t], ident[:], start=False, stop=(t == PACK - 1), is_transpose=True)
+            u_bf[r] = sb.tile([P, P, PACK], BF16, name=f"u_bf{r}", align_bytes=64)
+            nc.vector.scalar_tensor_tensor(u_bf[r][:], x_bank[r][:].rearrange("q t m -> q m t"), 0.0, along_slots(ra_t),
+                                           ALU.max, ALU.mult)
+
+        def multiply(r):
+            u_codes = sb.tile([P, P], U32, name=f"u_codes{r}", align_bytes=64)
+            u_scales = sb.tile([P, P], U8, name=f"u_scales{r}", align_bytes=64)
+            nc.vector.quantize_mx(u_codes[:].bitcast(E5M2X4), u_scales[:], u_bf[r][:].rearrange("q m t -> q (m t)"))
+            w_bank[r] = ps.tile([P, N], F32, name=f"w_bank{r}", tag=f"bank{r}")
+            nc.tensor.matmul_mx(w_bank[r][:], lhsT=u_codes[:].bitcast(E5M2X4), lhsT_scale=u_scales[:],
+                                rhs=g_codes[:].bitcast(E5M2X4), rhs_scale=g_scales[:], start=True, stop=True)
+
+        def offset(r):
+            part[r] = sb.tile([P, N], F32, name=f"part{r}", tag=f"x_pick{r + 1}")
+            neg_mean[r] = sb.tile([P, 1], F32, name=f"neg_mean{r}")
+            nc.vector.scalar_tensor_tensor(part[r][:], w_bank[r][:], -1.0 / N, bn_row[:].rearrange("q p e -> q (p e)"),
+                                           ALU.mult, ALU.add, accum_out=neg_mean[r][:])
+
+        def finish(r):
+            mag = sb.tile([P, N], BF16, name=f"mag{r}")
+            mag_sum = sb.tile([P, 1], F32, name=f"mag_sum{r}")
+            dw = sb.tile([P, N], F32, name=f"dw{r}")
+            nc.vector.tensor_scalar(dw[:], part[r][:], -float(N), neg_mean[r][:], ALU.mult, ALU.add)
+            if r == PACK - 1:
+                nc.scalar.activation(mag[:], part[r][:], ACT.Abs, bias=neg_mean[r][:], scale=-float(N), accum_out=mag_sum[:])
+            else:
+                nc.scalar.activation(mag[:], dw[:], ACT.Abs, accum_out=mag_sum[:])
+            den = sb.tile([P, 1], F32, name=f"den{r}")
+            nc.vector.tensor_scalar(den[:], mag_sum[:], 1.0 / N, 2.0, ALU.mult, ALU.add)
+            rec = sb.tile([P, 1], F32, name=f"rec{r}")
+            nc.vector.reciprocal(rec[:], den[:])
+            nc.vector.tensor_scalar(y[:, r, :], dw[:], rec[:], gk_t[:, r : r + 1], ALU.mult, ALU.mult)
+            nc.sync.dma_start(out_rows[:, r, :], y[:, r, :])
+
+        weigh(0)
+        multiply(0)
+        for r in range(1, PACK):
+            weigh(r)
+            offset(r - 1)
+            multiply(r)
+            finish(r - 1)
+        offset(PACK - 1)
+        finish(PACK - 1)
+
+        y_codes = sb.tile([P, N], U32, name="y_codes", align_bytes=64)
+        y_scales = sb.tile([P, N], U8, name="y_scales", align_bytes=64)
+        words_out = out_1[0].rearrange("l c r -> l (c r)").bitcast(I32)
+        for h in range(HALVES):
+            cols = slice(h * P, (h + 1) * P)
+            y_bf = sb.tile([P, P, PACK], BF16, name=f"y_bf{h}", align_bytes=64)
+            src = y[:, :, cols].rearrange("p r n -> p n r")
+            if h == 0:
+                nc.vector.tensor_copy(y_bf[:], src)
+            else:
+                nc.scalar.copy(y_bf[:], src)
+            nc.vector.quantize_mx(y_codes[:, cols].bitcast(E4M3X4), y_scales[:, cols], y_bf[:].rearrange("p n r -> p (n r)"))
+        nc.sync.dma_start(words_out, y_codes[:].bitcast(I32))
+        scales_out = out_2[0].bitcast(I32)
+        for q in range(4):
+            queue = nc.scalar if q % 2 == 0 else nc.sync
+            queue.dma_start(scales_out[4 * q : 4 * q + 4, :], y_scales[32 * q : 32 * q + 4, :].bitcast(I32))

@@ -41,10 +41,10 @@ def tile_list_moment_over_saved_spread_pl_kernel(tc, xf, ra, lo, gt, rb, sv, gk,
         xf_rows = xf.rearrange("(p r) t -> p r t", r=PACK)
 
         nc.sync.dma_start(lo_t[:], lo.rearrange("(p r) o -> p (r o)", r=PACK))
-        nc.scalar.dma_start(rb_t[:], rb[0].rearrange("(p t) -> p t", t=PACK))
-        nc.sync.dma_start(gt_win[0][:], gt[0:P, :])
         nc.scalar.dma_start(bn_t[:], bn[0].rearrange("(p e) -> p e", e=HALVES))
+        nc.sync.dma_start(gt_win[0][:], gt[0:P, :])
         nc.scalar.dma_start(ra_t[:], ra[0].rearrange("(p t) -> p t", t=PACK))
+        nc.scalar.dma_start(rb_t[:], rb[0].rearrange("(p t) -> p t", t=PACK))
         nc.sync.dma_start(list_g[:], offs2)
         nc.sync.dma_start(sv_win[0][:], sv[0:P, :])
         nc.sync.dma_start(sv_win[1][:], sv[P : 2 * P, :])
@@ -62,6 +62,17 @@ def tile_list_moment_over_saved_spread_pl_kernel(tc, xf, ra, lo, gt, rb, sv, gk,
 
         neg_lo = sb.tile([P, PACK], F32, name="neg_lo")
         nc.scalar.activation(neg_lo[:], lo_t[:], ACT.Copy, scale=-1.0)
+
+        x_bank = [ps.tile([P, PACK, P], F32, name=f"x_bank{r}", tag=f"bank{4 + r}") for r in range(PACK)]
+        for r in range(PACK):
+            for t in range(PACK):
+                nc.tensor.matmul(x_bank[r][:, t, :], neg_lo[:, r : r + 1].to_broadcast([P, P]), ident[:],
+                                 start=(t == 0), stop=False, is_transpose=True)
+        bn_bank = ps.tile([P, HALVES, P], F32, name="bn_bank", tag="bank3")
+        for e in range(HALVES):
+            nc.tensor.transpose(bn_bank[:, e, :], bn_t[:, e : e + 1].to_broadcast([P, P]), ident[:])
+        bn_row = sb.tile([P, P, HALVES], F32, name="bn_row")
+        nc.scalar.activation(bn_row[:], bn_bank[:].rearrange("q e p -> q p e"), ACT.Copy, scale=-1.0 / N)
 
         def pick_scalar(window, offsets, name):
             pick = sb.tile([P, J], F32, name=name, tag=name)
@@ -84,18 +95,7 @@ def tile_list_moment_over_saved_spread_pl_kernel(tc, xf, ra, lo, gt, rb, sv, gk,
         gt_turned = {0: turn(pick_scalar(gt_win[0], list_g, "gt_pick0"), "gt_bank0", "bank2")}
         sv_turned = {0: turn(pick_vector(sv_win[0], list_g, "sv_pick0"), "sv_bank0", "bank0")}
 
-        x_bank = [ps.tile([P, PACK, P], F32, name=f"x_bank{r}", tag=f"bank{4 + r}") for r in range(PACK)]
-        for r in range(PACK):
-            for t in range(PACK):
-                nc.tensor.matmul(x_bank[r][:, t, :], neg_lo[:, r : r + 1].to_broadcast([P, P]), ident[:],
-                                 start=(t == 0), stop=False, is_transpose=True)
-        bn_bank = ps.tile([P, HALVES, P], F32, name="bn_bank", tag="bank3")
-        for e in range(HALVES):
-            nc.tensor.transpose(bn_bank[:, e, :], bn_t[:, e : e + 1].to_broadcast([P, P]), ident[:])
-        bn_row = sb.tile([P, P, HALVES], F32, name="bn_row")
-        nc.vector.tensor_scalar(bn_row[:], bn_bank[:].rearrange("q e p -> q p e"), -1.0 / N, None, ALU.mult)
-
-        sv_turned[1] = turn(pick_scalar(sv_win[1], list_g, "sv_pick1"), "sv_bank1", "bank1")
+        sv_turned[1] = turn(pick_vector(sv_win[1], list_g, "sv_pick1"), "sv_bank1", "bank1")
         gt_turned[1] = turn(pick_scalar(gt_win[1], list_g, "gt_pick1"), "gt_bank1", "bank3")
         for h in range(HALVES):
             gate = sb.tile([P, P, PACK], F32, name=f"gate{h}")
@@ -107,55 +107,86 @@ def tile_list_moment_over_saved_spread_pl_kernel(tc, xf, ra, lo, gt, rb, sv, gk,
 
         y = sb.tile([P, PACK, N], F32, name="y")
         out_rows = out_0.rearrange("(p r) n -> p r n", r=PACK)
-        w_bank, u_bf, part, neg_mean = {}, {}, {}, {}
+        w_bank, part, dw, rec = {}, {}, {}, {}
+        neg_mean = [sb.tile([P, 2], F32, name=f"neg_mean{i}") for i in range(2)]
+        mag_sum = [sb.tile([P, 2], F32, name=f"mag_sum{i}") for i in range(2)]
 
-        def weigh(r):
+        def turn_x(r):
             slots = pick_scalar(x_win[r], list_x, f"x_pick{r}")
             for t in range(PACK):
                 nc.tensor.matmul(x_bank[r][:, t, :], slots[t], ident[:], start=False, stop=(t == PACK - 1), is_transpose=True)
-            u_bf[r] = sb.tile([P, P, PACK], BF16, name=f"u_bf{r}", align_bytes=64)
-            nc.vector.scalar_tensor_tensor(u_bf[r][:], x_bank[r][:].rearrange("q t m -> q m t"), 0.0, along_slots(ra_t),
-                                           ALU.max, ALU.mult)
 
         def multiply(r):
+            u_bf = sb.tile([P, P, PACK], BF16, name=f"u_bf{r}", tag=f"u_bf{r}", align_bytes=64)
+            nc.vector.scalar_tensor_tensor(u_bf[:], x_bank[r][:].rearrange("q t m -> q m t"), 0.0, along_slots(ra_t),
+                                           ALU.max, ALU.mult)
             u_codes = sb.tile([P, P], U32, name=f"u_codes{r}", align_bytes=64)
             u_scales = sb.tile([P, P], U8, name=f"u_scales{r}", align_bytes=64)
-            nc.vector.quantize_mx(u_codes[:].bitcast(E5M2X4), u_scales[:], u_bf[r][:].rearrange("q m t -> q (m t)"))
+            nc.vector.quantize_mx(u_codes[:].bitcast(E5M2X4), u_scales[:], u_bf[:].rearrange("q m t -> q (m t)"))
             w_bank[r] = ps.tile([P, N], F32, name=f"w_bank{r}", tag=f"bank{r}")
             nc.tensor.matmul_mx(w_bank[r][:], lhsT=u_codes[:].bitcast(E5M2X4), lhsT_scale=u_scales[:],
                                 rhs=g_codes[:].bitcast(E5M2X4), rhs_scale=g_scales[:], start=True, stop=True)
 
+        def column(pair_tiles, r):
+            return pair_tiles[r // 2][:, r % 2 : r % 2 + 1]
+
         def offset(r):
-            part[r] = sb.tile([P, N], F32, name=f"part{r}", tag=f"x_pick{r + 1}")
-            neg_mean[r] = sb.tile([P, 1], F32, name=f"neg_mean{r}")
+            part[r] = sb.tile([P, N], F32, name=f"part{r}", tag=f"u_bf{r + 1}", align_bytes=64)
             nc.vector.scalar_tensor_tensor(part[r][:], w_bank[r][:], -1.0 / N, bn_row[:].rearrange("q p e -> q (p e)"),
-                                           ALU.mult, ALU.add, accum_out=neg_mean[r][:])
+                                           ALU.mult, ALU.add, accum_out=column(neg_mean, r))
 
-        def finish(r):
+        def spread(r):
             mag = sb.tile([P, N], BF16, name=f"mag{r}")
-            mag_sum = sb.tile([P, 1], F32, name=f"mag_sum{r}")
-            dw = sb.tile([P, N], F32, name=f"dw{r}")
-            nc.vector.tensor_scalar(dw[:], part[r][:], -float(N), neg_mean[r][:], ALU.mult, ALU.add)
-            if r == PACK - 1:
-                nc.scalar.activation(mag[:], part[r][:], ACT.Abs, bias=neg_mean[r][:], scale=-float(N), accum_out=mag_sum[:])
-            else:
-                nc.scalar.activation(mag[:], dw[:], ACT.Abs, accum_out=mag_sum[:])
-            den = sb.tile([P, 1], F32, name=f"den{r}")
-            nc.vector.tensor_scalar(den[:], mag_sum[:], 1.0 / N, 2.0, ALU.mult, ALU.add)
-            rec = sb.tile([P, 1], F32, name=f"rec{r}")
-            nc.vector.reciprocal(rec[:], den[:])
-            nc.vector.tensor_scalar(y[:, r, :], dw[:], rec[:], gk_t[:, r : r + 1], ALU.mult, ALU.mult)
-            nc.sync.dma_start(out_rows[:, r, :], y[:, r, :])
+            nc.scalar.activation(mag[:], part[r][:], ACT.Abs, bias=column(neg_mean, r), scale=-float(N),
+                                 accum_out=column(mag_sum, r))
 
-        weigh(0)
-        multiply(0)
-        for r in range(1, PACK):
-            weigh(r)
-            offset(r - 1)
+        def inverse(i):
+            den = sb.tile([P, 2], F32, name=f"den{i}")
+            nc.vector.tensor_scalar(den[:], mag_sum[i][:], 1.0 / N, 2.0, ALU.mult, ALU.add)
+            rec[i] = sb.tile([P, 2], F32, name=f"rec{i}")
+            nc.vector.reciprocal(rec[i][:], den[:])
+
+        def store(i):
+            nc.sync.dma_start(out_rows[:, 2 * i : 2 * i + 2, :], y[:, 2 * i : 2 * i + 2, :])
+
+        def finish_on_scalar(i):
+            inverse(i)
+            gk_pair = gk_t[:, 2 * i : 2 * i + 2]
+            terms = sb.tile([P, 2, 2], F32, name="terms")
+            nc.vector.tensor_scalar(terms[:, 0, :], gk_pair, -float(N), None, ALU.mult)
+            nc.vector.tensor_tensor(terms[:, 1, :], neg_mean[i][:], gk_pair, ALU.mult)
+            line = sb.tile([P, 2, 2], F32, name="line")
+            nc.vector.tensor_tensor(line[:], terms[:], rec[i][:].unsqueeze(1).to_broadcast([P, 2, 2]), ALU.mult)
+            for c in range(2):
+                nc.scalar.activation(y[:, 2 * i + c, :], part[2 * i + c][:], ACT.Identity,
+                                     bias=line[:, 1, c : c + 1], scale=line[:, 0, c : c + 1])
+            store(i)
+
+        def centre(r):
+            dw[r] = sb.tile([P, N], F32, name=f"dw{r}")
+            nc.vector.tensor_scalar(dw[r][:], part[r][:], -float(N), column(neg_mean, r), ALU.mult, ALU.add)
+
+        def finish_on_vector(i):
+            inverse(i)
+            for r in (2 * i, 2 * i + 1):
+                nc.vector.tensor_scalar(y[:, r, :], dw[r][:], column(rec, r), gk_t[:, r : r + 1], ALU.mult, ALU.mult)
+            store(i)
+
+        for r in range(PACK):
+            turn_x(r)
+        for r in range(PACK):
             multiply(r)
-            finish(r - 1)
-        offset(PACK - 1)
-        finish(PACK - 1)
+        for r in (0, 1):
+            offset(r)
+            spread(r)
+        offset(2)
+        finish_on_scalar(0)
+        spread(2)
+        centre(2)
+        offset(3)
+        spread(3)
+        centre(3)
+        finish_on_vector(1)
 
         y_codes = sb.tile([P, N], U32, name="y_codes", align_bytes=64)
         y_scales = sb.tile([P, N], U8, name="y_scales", align_bytes=64)

@@ -37,11 +37,11 @@ def tile_list_moment_over_saved_spread_pl_kernel(tc, xf, ra, lo, gt, rb, sv, gk,
         rb_t = sb.tile([P, PACK], F32, name="rb_t")
         lo_t = sb.tile([P, PACK], F32, name="lo_t")
         gk_t = sb.tile([P, PACK], F32, name="gk_t")
-        bn_t = sb.tile([P, HALVES], F32, name="bn_t")
+        bn_row = sb.tile([P, N], F32, name="bn_row")
         xf_rows = xf.rearrange("(p r) t -> p r t", r=PACK)
 
         nc.sync.dma_start(lo_t[:], lo.rearrange("(p r) o -> p (r o)", r=PACK))
-        nc.scalar.dma_start(bn_t[:], bn[0].rearrange("(p e) -> p e", e=HALVES))
+        nc.scalar.dma_start(gk_t[:], gk.rearrange("(p r) o -> p (r o)", r=PACK))
         nc.sync.dma_start(gt_win[0][:], gt[0:P, :])
         nc.scalar.dma_start(ra_t[:], ra[0].rearrange("(p t) -> p t", t=PACK))
         nc.scalar.dma_start(rb_t[:], rb[0].rearrange("(p t) -> p t", t=PACK))
@@ -52,7 +52,7 @@ def tile_list_moment_over_saved_spread_pl_kernel(tc, xf, ra, lo, gt, rb, sv, gk,
         nc.sync.dma_start(list_x[:], offs)
         for r in range(PACK):
             nc.sync.dma_start(x_win[r][:], xf_rows[:, r, :])
-        nc.sync.dma_start(gk_t[:], gk.rearrange("(p r) o -> p (r o)", r=PACK))
+        nc.sync.dma_start(bn_row[:], bn[0].partition_broadcast(P))
 
         ident = sb.tile([P, P], F32, name="ident")
         make_identity(nc, ident[:])
@@ -68,11 +68,6 @@ def tile_list_moment_over_saved_spread_pl_kernel(tc, xf, ra, lo, gt, rb, sv, gk,
             for t in range(PACK):
                 nc.tensor.matmul(x_bank[r][:, t, :], neg_lo[:, r : r + 1].to_broadcast([P, P]), ident[:],
                                  start=(t == 0), stop=False, is_transpose=True)
-        bn_bank = ps.tile([P, HALVES, P], F32, name="bn_bank", tag="bank3")
-        for e in range(HALVES):
-            nc.tensor.transpose(bn_bank[:, e, :], bn_t[:, e : e + 1].to_broadcast([P, P]), ident[:])
-        bn_row = sb.tile([P, P, HALVES], F32, name="bn_row")
-        nc.scalar.activation(bn_row[:], bn_bank[:].rearrange("q e p -> q p e"), ACT.Copy, scale=-1.0 / N)
 
         def pick_scalar(window, offsets, name):
             pick = sb.tile([P, J], F32, name=name, tag=name)
@@ -108,7 +103,7 @@ def tile_list_moment_over_saved_spread_pl_kernel(tc, xf, ra, lo, gt, rb, sv, gk,
         y = sb.tile([P, PACK, N], F32, name="y")
         out_rows = out_0.rearrange("(p r) n -> p r n", r=PACK)
         w_bank, part, dw, rec = {}, {}, {}, {}
-        neg_mean = [sb.tile([P, 2], F32, name=f"neg_mean{i}") for i in range(2)]
+        row_sum = [sb.tile([P, 2], F32, name=f"row_sum{i}") for i in range(2)]
         mag_sum = [sb.tile([P, 2], F32, name=f"mag_sum{i}") for i in range(2)]
 
         def turn_x(r):
@@ -131,18 +126,18 @@ def tile_list_moment_over_saved_spread_pl_kernel(tc, xf, ra, lo, gt, rb, sv, gk,
             return pair_tiles[r // 2][:, r % 2 : r % 2 + 1]
 
         def offset(r):
-            part[r] = sb.tile([P, N], F32, name=f"part{r}", tag=f"u_bf{r + 1}", align_bytes=64)
-            nc.vector.scalar_tensor_tensor(part[r][:], w_bank[r][:], -1.0 / N, bn_row[:].rearrange("q p e -> q (p e)"),
-                                           ALU.mult, ALU.add, accum_out=column(neg_mean, r))
+            part[r] = sb.tile([P, N], F32, name=f"part{r}")
+            nc.vector.scalar_tensor_tensor(part[r][:], w_bank[r][:], 1.0, bn_row[:],
+                                           ALU.mult, ALU.add, accum_out=column(row_sum, r))
 
         def spread(r):
             mag = sb.tile([P, N], BF16, name=f"mag{r}")
-            nc.scalar.activation(mag[:], part[r][:], ACT.Abs, bias=column(neg_mean, r), scale=-float(N),
+            nc.scalar.activation(mag[:], part[r][:], ACT.Abs, bias=column(row_sum, r), scale=-float(N),
                                  accum_out=column(mag_sum, r))
 
         def inverse(i):
             den = sb.tile([P, 2], F32, name=f"den{i}")
-            nc.vector.tensor_scalar(den[:], mag_sum[i][:], 1.0 / N, 2.0, ALU.mult, ALU.add)
+            nc.vector.tensor_scalar(den[:], mag_sum[i][:], -1.0 / N, -2.0 * N, ALU.mult, ALU.add)
             rec[i] = sb.tile([P, 2], F32, name=f"rec{i}")
             nc.vector.reciprocal(rec[i][:], den[:])
 
@@ -154,7 +149,7 @@ def tile_list_moment_over_saved_spread_pl_kernel(tc, xf, ra, lo, gt, rb, sv, gk,
             gk_pair = gk_t[:, 2 * i : 2 * i + 2]
             terms = sb.tile([P, 2, 2], F32, name="terms")
             nc.vector.tensor_scalar(terms[:, 0, :], gk_pair, -float(N), None, ALU.mult)
-            nc.vector.tensor_tensor(terms[:, 1, :], neg_mean[i][:], gk_pair, ALU.mult)
+            nc.vector.tensor_tensor(terms[:, 1, :], row_sum[i][:], gk_pair, ALU.mult)
             line = sb.tile([P, 2, 2], F32, name="line")
             nc.vector.tensor_tensor(line[:], terms[:], rec[i][:].unsqueeze(1).to_broadcast([P, 2, 2]), ALU.mult)
             for c in range(2):
@@ -164,7 +159,7 @@ def tile_list_moment_over_saved_spread_pl_kernel(tc, xf, ra, lo, gt, rb, sv, gk,
 
         def centre(r):
             dw[r] = sb.tile([P, N], F32, name=f"dw{r}")
-            nc.vector.tensor_scalar(dw[r][:], part[r][:], -float(N), column(neg_mean, r), ALU.mult, ALU.add)
+            nc.vector.tensor_scalar(dw[r][:], part[r][:], -float(N), column(row_sum, r), ALU.mult, ALU.add)
 
         def finish_on_vector(i):
             inverse(i)

@@ -37,22 +37,22 @@ def tile_list_moment_over_saved_spread_pl_kernel(tc, xf, ra, lo, gt, rb, sv, gk,
         rb_t = sb.tile([P, PACK], F32, name="rb_t")
         lo_t = sb.tile([P, PACK], F32, name="lo_t")
         gk_t = sb.tile([P, PACK], F32, name="gk_t")
-        bn_row = sb.tile([P, N], F32, name="bn_row")
+        bn_t = sb.tile([P, HALVES], F32, name="bn_t")
         xf_rows = xf.rearrange("(p r) t -> p r t", r=PACK)
 
         nc.sync.dma_start(lo_t[:], lo.rearrange("(p r) o -> p (r o)", r=PACK))
-        nc.scalar.dma_start(gk_t[:], gk.rearrange("(p r) o -> p (r o)", r=PACK))
+        nc.scalar.dma_start(bn_t[:], bn[0].rearrange("(p e) -> p e", e=HALVES))
         nc.sync.dma_start(gt_win[0][:], gt[0:P, :])
         nc.scalar.dma_start(ra_t[:], ra[0].rearrange("(p t) -> p t", t=PACK))
         nc.scalar.dma_start(rb_t[:], rb[0].rearrange("(p t) -> p t", t=PACK))
         nc.sync.dma_start(list_g[:], offs2)
         nc.sync.dma_start(sv_win[0][:], sv[0:P, :])
         nc.sync.dma_start(sv_win[1][:], sv[P : 2 * P, :])
+        nc.sync.dma_start(gk_t[:], gk.rearrange("(p r) o -> p (r o)", r=PACK))
         nc.sync.dma_start(gt_win[1][:], gt[P : 2 * P, :])
         nc.sync.dma_start(list_x[:], offs)
         for r in range(PACK):
             nc.sync.dma_start(x_win[r][:], xf_rows[:, r, :])
-        nc.sync.dma_start(bn_row[:], bn[0].partition_broadcast(P))
 
         ident = sb.tile([P, P], F32, name="ident")
         make_identity(nc, ident[:])
@@ -63,21 +63,25 @@ def tile_list_moment_over_saved_spread_pl_kernel(tc, xf, ra, lo, gt, rb, sv, gk,
         neg_lo = sb.tile([P, PACK], F32, name="neg_lo")
         nc.scalar.activation(neg_lo[:], lo_t[:], ACT.Copy, scale=-1.0)
 
+        bn_bank = ps.tile([P, HALVES, P], F32, name="bn_bank", tag="bank3")
+        for e in range(HALVES):
+            nc.tensor.transpose(bn_bank[:, e, :], bn_t[:, e : e + 1].to_broadcast([P, P]), ident[:])
+        bn_row = sb.tile([P, P, HALVES], F32, name="bn_row")
+        nc.vector.tensor_copy(bn_row[:], bn_bank[:].rearrange("q e p -> q p e"))
         x_bank = [ps.tile([P, PACK, P], F32, name=f"x_bank{r}", tag=f"bank{4 + r}") for r in range(PACK)]
         for r in range(PACK):
             for t in range(PACK):
                 nc.tensor.matmul(x_bank[r][:, t, :], neg_lo[:, r : r + 1].to_broadcast([P, P]), ident[:],
                                  start=(t == 0), stop=False, is_transpose=True)
 
-        def pick_scalar(window, offsets, name):
-            pick = sb.tile([P, J], F32, name=name, tag=name)
-            nc.scalar.activation(pick[:], window[:].indirect(offsets[:]), ACT.Copy)
-            return [pick[:, t::PACK] for t in range(PACK)]
-
-        def pick_vector(window, offsets, name):
-            pick = sb.tile([P, PACK, P], F32, name=name, tag=name)
-            nc.vector.tensor_copy(pick[:].rearrange("p t q -> p q t"), window[:].indirect(offsets[:]))
-            return [pick[:, t, :] for t in range(PACK)]
+        def pick(window, offsets, name, vector_columns, tag=None):
+            picked = sb.tile([P, J], F32, name=name, tag=tag or name)
+            cut = 16 * vector_columns
+            if vector_columns < J // 16:
+                nc.scalar.activation(picked[:, cut:], window[:].indirect(offsets[:, vector_columns:]), ACT.Copy)
+            if vector_columns > 0:
+                nc.vector.tensor_copy(picked[:, :cut], window[:].indirect(offsets[:, :vector_columns]))
+            return [picked[:, t::PACK] for t in range(PACK)]
 
         def turn(slots, name, tag):
             bank = ps.tile([P, PACK, P], F32, name=name, tag=tag)
@@ -87,13 +91,13 @@ def tile_list_moment_over_saved_spread_pl_kernel(tc, xf, ra, lo, gt, rb, sv, gk,
 
         g_codes = sb.tile([P, N], U32, name="g_codes", align_bytes=64)
         g_scales = sb.tile([P, N], U8, name="g_scales", align_bytes=64)
-        gt_turned = {0: turn(pick_scalar(gt_win[0], list_g, "gt_pick0"), "gt_bank0", "bank2")}
-        sv_turned = {0: turn(pick_vector(sv_win[0], list_g, "sv_pick0"), "sv_bank0", "bank0")}
+        gt_turned = {0: turn(pick(gt_win[0], list_g, "gt_pick0", 0), "gt_bank0", "bank2")}
+        sv_turned = {0: turn(pick(sv_win[0], list_g, "sv_pick0", J // 16), "sv_bank0", "bank0")}
 
-        sv_turned[1] = turn(pick_vector(sv_win[1], list_g, "sv_pick1"), "sv_bank1", "bank1")
-        gt_turned[1] = turn(pick_scalar(gt_win[1], list_g, "gt_pick1"), "gt_bank1", "bank3")
+        sv_turned[1] = turn(pick(sv_win[1], list_g, "sv_pick1", J // 16), "sv_bank1", "bank1")
+        gt_turned[1] = turn(pick(gt_win[1], list_g, "gt_pick1", 0), "gt_bank1", "bank3")
         for h in range(HALVES):
-            gate = sb.tile([P, P, PACK], F32, name=f"gate{h}")
+            gate = sb.tile([P, P, PACK], F32, name=f"gate{h}", tag=f"gate{h}")
             nc.vector.scalar_tensor_tensor(gate[:], sv_turned[h], 0.0, along_slots(rb_t), ALU.max, ALU.mult)
             g_bf = sb.tile([P, P, PACK], BF16, name=f"g_bf{h}", align_bytes=64)
             nc.vector.tensor_tensor(g_bf[:], gt_turned[h], gate[:], ALU.mult)
@@ -107,7 +111,8 @@ def tile_list_moment_over_saved_spread_pl_kernel(tc, xf, ra, lo, gt, rb, sv, gk,
         mag_sum = [sb.tile([P, 2], F32, name=f"mag_sum{i}") for i in range(2)]
 
         def turn_x(r):
-            slots = pick_scalar(x_win[r], list_x, f"x_pick{r}")
+            shared = r >= PACK - HALVES
+            slots = pick(x_win[r], list_x, f"x_pick{r}", 10 if shared else 0, f"gate{r - (PACK - HALVES)}" if shared else None)
             for t in range(PACK):
                 nc.tensor.matmul(x_bank[r][:, t, :], slots[t], ident[:], start=False, stop=(t == PACK - 1), is_transpose=True)
 
@@ -127,7 +132,7 @@ def tile_list_moment_over_saved_spread_pl_kernel(tc, xf, ra, lo, gt, rb, sv, gk,
 
         def offset(r):
             part[r] = sb.tile([P, N], F32, name=f"part{r}")
-            nc.vector.scalar_tensor_tensor(part[r][:], w_bank[r][:], 1.0, bn_row[:],
+            nc.vector.scalar_tensor_tensor(part[r][:], w_bank[r][:], 1.0, bn_row[:].rearrange("q p e -> q (p e)"),
                                            ALU.mult, ALU.add, accum_out=column(row_sum, r))
 
         def spread(r):

@@ -94,8 +94,8 @@ def tile_list_moment_over_saved_spread_pl_kernel(tc, xf, ra, lo, gt, rb, sv, gk,
         gt_turned = {0: turn(pick(gt_win[0], list_g, "gt_pick0", 0), "gt_bank0", "bank2")}
         sv_turned = {0: turn(pick(sv_win[0], list_g, "sv_pick0", J // 16), "sv_bank0", "bank0")}
 
-        sv_turned[1] = turn(pick(sv_win[1], list_g, "sv_pick1", J // 16), "sv_bank1", "bank1")
-        gt_turned[1] = turn(pick(gt_win[1], list_g, "gt_pick1", 0), "gt_bank1", "bank3")
+        sv_turned[1] = turn(pick(sv_win[1], list_g, "sv_pick1", 16), "sv_bank1", "bank1")
+        gt_turned[1] = turn(pick(gt_win[1], list_g, "gt_pick1", 16), "gt_bank1", "bank3")
         for h in range(HALVES):
             gate = sb.tile([P, P, PACK], F32, name=f"gate{h}", tag=f"gate{h}")
             nc.vector.scalar_tensor_tensor(gate[:], sv_turned[h], 0.0, along_slots(rb_t), ALU.max, ALU.mult)
@@ -112,7 +112,7 @@ def tile_list_moment_over_saved_spread_pl_kernel(tc, xf, ra, lo, gt, rb, sv, gk,
 
         def turn_x(r):
             shared = r >= PACK - HALVES
-            slots = pick(x_win[r], list_x, f"x_pick{r}", 10 if shared else 0, f"gate{r - (PACK - HALVES)}" if shared else None)
+            slots = pick(x_win[r], list_x, f"x_pick{r}", 16 if shared else 0, f"gate{r - (PACK - HALVES)}" if shared else None)
             for t in range(PACK):
                 nc.tensor.matmul(x_bank[r][:, t, :], slots[t], ident[:], start=False, stop=(t == PACK - 1), is_transpose=True)
 
@@ -194,11 +194,12 @@ def tile_list_moment_over_saved_spread_pl_kernel(tc, xf, ra, lo, gt, rb, sv, gk,
         for h in range(HALVES):
             cols = slice(h * P, (h + 1) * P)
             y_bf = sb.tile([P, P, PACK], BF16, name=f"y_bf{h}", align_bytes=64)
-            src = y[:, :, cols].rearrange("p r n -> p n r")
+            src = y[:, :, cols].rearrange("p r (c i) -> p c r i", i=4)
+            dst = y_bf[:].rearrange("p (c i) r -> p c r i", i=4)
             if h == 0:
-                nc.vector.tensor_copy(y_bf[:], src)
+                nc.vector.tensor_copy(dst, src)
             else:
-                nc.scalar.copy(y_bf[:], src)
+                nc.scalar.copy(dst, src)
             nc.vector.quantize_mx(y_codes[:, cols].bitcast(E4M3X4), y_scales[:, cols], y_bf[:].rearrange("p n r -> p (n r)"))
         nc.sync.dma_start(words_out, y_codes[:].bitcast(I32))
         scales_out = out_2[0].bitcast(I32)

from contextlib import ExitStack

import concourse.mybir as mybir
from concourse.masks import make_identity

K, J, N, T, V = 512, 512, 256, 1024, 1024
FLOPS = 2 * K * J * N

F32 = mybir.dt.float32
BF16 = mybir.dt.bfloat16
U32 = mybir.dt.uint32
I32 = mybir.dt.int32
U16 = mybir.dt.uint16
U8 = mybir.dt.uint8
E5M2X4 = mybir.dt.float8_e5m2_x4
E4M3X4 = mybir.dt.float8_e4m3fn_x4
ALU = mybir.AluOpType
ACT = mybir.ActivationFunctionType

P = 128
PACK = 4
HALVES = N // P


def tile_list_moment_over_saved_spread_pl_kernel(tc, xf, ra, lo, gt, rb, sv, gk, bn, offs, offs2, out_0, out_1, out_2):
    nc = tc.nc
    with ExitStack() as ctx:
        sb = ctx.enter_context(tc.tile_pool(name="sb", bufs=1))
        ps = ctx.enter_context(tc.psum_pool(name="ps", bufs=1))

        list_x = sb.tile([P, J // 16], U16, name="list_x")
        list_g = sb.tile([P, J // 16], U16, name="list_g")
        sv_win = [sb.tile([P, V], F32, name=f"sv_win{h}") for h in range(HALVES)]
        gt_win = [sb.tile([P, V], F32, name=f"gt_win{h}") for h in range(HALVES)]
        x_win = [sb.tile([P, T], F32, name=f"x_win{r}") for r in range(PACK)]
        ra_t = sb.tile([P, PACK], F32, name="ra_t")
        rb_t = sb.tile([P, PACK], F32, name="rb_t")
        lo_t = sb.tile([P, PACK], F32, name="lo_t")
        gk_t = sb.tile([P, PACK], F32, name="gk_t")
        bn_t = sb.tile([P, HALVES], F32, name="bn_t")
        xf_rows = xf.rearrange("(p r) t -> p r t", r=PACK)

        nc.sync.dma_start(lo_t[:], lo.rearrange("(p r) o -> p (r o)", r=PACK))
        nc.scalar.dma_start(bn_t[:], bn[0].rearrange("(p e) -> p e", e=HALVES))
        nc.sync.dma_start(gt_win[0][:], gt[0:P, :])
        nc.scalar.dma_start(ra_t[:], ra[0].rearrange("(p t) -> p t", t=PACK))
        nc.scalar.dma_start(rb_t[:], rb[0].rearrange("(p t) -> p t", t=PACK))
        nc.sync.dma_start(list_g[:], offs2)
        nc.sync.dma_start(sv_win[0][:], sv[0:P, :])
        nc.sync.dma_start(sv_win[1][:], sv[P : 2 * P, :])
        nc.sync.dma_start(gk_t[:], gk.rearrange("(p r) o -> p (r o)", r=PACK))
        nc.sync.dma_start(gt_win[1][:], gt[P : 2 * P, :])
        nc.sync.dma_start(list_x[:], offs)
        for r in range(PACK):
            nc.sync.dma_start(x_win[r][:], xf_rows[:, r, :])

        ident = sb.tile([P, P], F32, name="ident")
        make_identity(nc, ident[:])

        def along_slots(weights):
            return weights[:].unsqueeze(1).to_broadcast([P, P, PACK])

        neg_lo = sb.tile([P, PACK], F32, name="neg_lo")
        nc.scalar.activation(neg_lo[:], lo_t[:], ACT.Copy, scale=-1.0)

        bn_bank = ps.tile([P, HALVES, P], F32, name="bn_bank", tag="bank3")
        for e in range(HALVES):
            nc.tensor.transpose(bn_bank[:, e, :], bn_t[:, e : e + 1].to_broadcast([P, P]), ident[:])
        bn_row = sb.tile([P, P, HALVES], F32, name="bn_row")
        nc.vector.tensor_copy(bn_row[:], bn_bank[:].rearrange("q e p -> q p e"))
        x_bank = [ps.tile([P, PACK, P], F32, name=f"x_bank{r}", tag=f"bank{4 + r}") for r in range(PACK)]
        for r in range(PACK):
            for t in range(PACK):
                nc.tensor.matmul(x_bank[r][:, t, :], neg_lo[:, r : r + 1].to_broadcast([P, P]), ident[:],
                                 start=(t == 0), stop=False, is_transpose=True)

        def pick(window, offsets, name, vector_columns, tag=None):
            picked = sb.tile([P, J], F32, name=name, tag=tag or name)
            cut = 16 * vector_columns
            if vector_columns < J // 16:
                nc.scalar.activation(picked[:, cut:], window[:].indirect(offsets[:, vector_columns:]), ACT.Copy)
            if vector_columns > 0:
                nc.vector.tensor_copy(picked[:, :cut], window[:].indirect(offsets[:, :vector_columns]))
            return [picked[:, t::PACK] for t in range(PACK)]

        def turn(slots, name, tag):
            bank = ps.tile([P, PACK, P], F32, name=name, tag=tag)
            for t in range(PACK):
                nc.tensor.transpose(bank[:, t, :], slots[t], ident[:])
            return bank[:].rearrange("q t m -> q m t")

        g_codes = sb.tile([P, N], U32, name="g_codes", align_bytes=64)
        g_scales = sb.tile([P, N], U8, name="g_scales", align_bytes=64)
        gt_turned = {0: turn(pick(gt_win[0], list_g, "gt_pick0", 0), "gt_bank0", "bank2")}
        sv_turned = {0: turn(pick(sv_win[0], list_g, "sv_pick0", J // 16), "sv_bank0", "bank0")}

        sv_turned[1] = turn(pick(sv_win[1], list_g, "sv_pick1", 16), "sv_bank1", "bank1")
        gt_turned[1] = turn(pick(gt_win[1], list_g, "gt_pick1", 16), "gt_bank1", "bank3")
        for h in range(HALVES):
            gate = sb.tile([P, P, PACK], F32, name=f"gate{h}", tag=f"gate{h}")
            nc.vector.scalar_tensor_tensor(gate[:], sv_turned[h], 0.0, along_slots(rb_t), ALU.max, ALU.mult)
            g_bf = sb.tile([P, P, PACK], BF16, name=f"g_bf{h}", align_bytes=64)
            nc.vector.tensor_tensor(g_bf[:], gt_turned[h], gate[:], ALU.mult)
            cols = slice(h * P, (h + 1) * P)
            nc.vector.quantize_mx(g_codes[:, cols].bitcast(E5M2X4), g_scales[:, cols], g_bf[:].rearrange("q m t -> q (m t)"))

        y = sb.tile([P, PACK, N], F32, name="y")
        out_rows = out_0.rearrange("(p r) n -> p r n", r=PACK)
        w_bank, part, dw, rec = {}, {}, {}, {}
        row_sum = [sb.tile([P, 2], F32, name=f"row_sum{i}") for i in range(2)]
        mag_sum = [sb.tile([P, 2], F32, name=f"mag_sum{i}") for i in range(2)]

        def turn_x(r):
            shared = r >= PACK - HALVES
            slots = pick(x_win[r], list_x, f"x_pick{r}", 16 if shared else 0, f"gate{r - (PACK - HALVES)}" if shared else None)
            for t in range(PACK):
                nc.tensor.matmul(x_bank[r][:, t, :], slots[t], ident[:], start=False, stop=(t == PACK - 1), is_transpose=True)

        def multiply(r):
            u_bf = sb.tile([P, P, PACK], BF16, name=f"u_bf{r}", tag=f"u_bf{r}", align_bytes=64)
            nc.vector.scalar_tensor_tensor(u_bf[:], x_bank[r][:].rearrange("q t m -> q m t"), 0.0, along_slots(ra_t),
                                           ALU.max, ALU.mult)
            u_codes = sb.tile([P, P], U32, name=f"u_codes{r}", align_bytes=64)
            u_scales = sb.tile([P, P], U8, name=f"u_scales{r}", align_bytes=64)
            nc.vector.quantize_mx(u_codes[:].bitcast(E5M2X4), u_scales[:], u_bf[:].rearrange("q m t -> q (m t)"))
            w_bank[r] = ps.tile([P, N], F32, name=f"w_bank{r}", tag=f"bank{r}")
            nc.tensor.matmul_mx(w_bank[r][:], lhsT=u_codes[:].bitcast(E5M2X4), lhsT_scale=u_scales[:],
                                rhs=g_codes[:].bitcast(E5M2X4), rhs_scale=g_scales[:], start=True, stop=True)

        def column(pair_tiles, r):
            return pair_tiles[r // 2][:, r % 2 : r % 2 + 1]

        def offset(r):
            part[r] = sb.tile([P, N], F32, name=f"part{r}")
            nc.vector.scalar_tensor_tensor(part[r][:], w_bank[r][:], 1.0, bn_row[:].rearrange("q p e -> q (p e)"),
                                           ALU.mult, ALU.add, accum_out=column(row_sum, r))

        def spread(r):
            mag = sb.tile([P, N], BF16, name=f"mag{r}")
            nc.scalar.activation(mag[:], part[r][:], ACT.Abs, bias=column(row_sum, r), scale=-float(N),
                                 accum_out=column(mag_sum, r))

        def inverse(i):
            den = sb.tile([P, 2], F32, name=f"den{i}")
            nc.vector.tensor_scalar(den[:], mag_sum[i][:], -1.0 / N, -2.0 * N, ALU.mult, ALU.add)
            rec[i] = sb.tile([P, 2], F32, name=f"rec{i}")
            nc.vector.reciprocal(rec[i][:], den[:])

        def store(i):
            nc.sync.dma_start(out_rows[:, 2 * i : 2 * i + 2, :], y[:, 2 * i : 2 * i + 2, :])

        def finish_on_scalar(i):
            inverse(i)
            gk_pair = gk_t[:, 2 * i : 2 * i + 2]
            terms = sb.tile([P, 2, 2], F32, name="terms")
            nc.vector.tensor_scalar(terms[:, 0, :], gk_pair, -float(N), None, ALU.mult)
            nc.vector.tensor_tensor(terms[:, 1, :], row_sum[i][:], gk_pair, ALU.mult)
            line = sb.tile([P, 2, 2], F32, name="line")
            nc.vector.tensor_tensor(line[:], terms[:], rec[i][:].unsqueeze(1).to_broadcast([P, 2, 2]), ALU.mult)
            for c in range(2):
                nc.scalar.activation(y[:, 2 * i + c, :], part[2 * i + c][:], ACT.Identity,
                                     bias=line[:, 1, c : c + 1], scale=line[:, 0, c : c + 1])
            store(i)

        def centre(r):
            dw[r] = sb.tile([P, N], F32, name=f"dw{r}")
            nc.vector.tensor_scalar(dw[r][:], part[r][:], -float(N), column(row_sum, r), ALU.mult, ALU.add)

        def finish_on_vector(i):
            inverse(i)
            for r in (2 * i, 2 * i + 1):
                nc.vector.tensor_scalar(y[:, r, :], dw[r][:], column(rec, r), gk_t[:, r : r + 1], ALU.mult, ALU.mult)
            store(i)

        for r in range(PACK):
            turn_x(r)
        for r in range(PACK):
            multiply(r)
        for r in (0, 1):
            offset(r)
            spread(r)
        offset(2)
        finish_on_scalar(0)
        spread(2)
        centre(2)
        offset(3)
        spread(3)
        centre(3)
        finish_on_vector(1)

        y_codes = sb.tile([P, N], U32, name="y_codes", align_bytes=64)
        y_scales = sb.tile([P, N], U8, name="y_scales", align_bytes=64)
        words_out = out_1[0].rearrange("l c r -> l (c r)").bitcast(I32)
        for h in range(HALVES):
            cols = slice(h * P, (h + 1) * P)
            y_bf = sb.tile([P, P, PACK], BF16, name=f"y_bf{h}", align_bytes=64)
            src = y[:, :, cols].rearrange("p r (c i) -> p c r i", i=4)
            dst = y_bf[:].rearrange("p (c i) r -> p c r i", i=4)
            if h == 0:
                nc.vector.tensor_copy(dst, src)
            else:
                nc.scalar.copy(dst, src)
            nc.vector.quantize_mx(y_codes[:, cols].bitcast(E4M3X4), y_scales[:, cols], y_bf[:].rearrange("p n r -> p (n r)"))
        nc.sync.dma_start(words_out, y_codes[:].bitcast(I32))
        scales_out = out_2[0].bitcast(I32)
        for q in range(4):
            queue = nc.scalar if q % 2 == 0 else nc.sync
            queue.dma_start(scales_out[4 * q : 4 * q + 4, :], y_scales[32 * q : 32 * q + 4, :].bitcast(I32))
